import numpy as np
import ml_dtypes


def mxq(x, axis, fmt="e4m3"):
    dtype, down = {"e4m3": (ml_dtypes.float8_e4m3fn, 7), "e5m2": (ml_dtypes.float8_e5m2, 14)}[fmt]
    v = np.moveaxis(np.asarray(x, np.float32).astype(ml_dtypes.bfloat16).astype(np.float64), axis, -1)
    blocks = v.reshape(v.shape[:-1] + (-1, 32))
    amax = np.abs(blocks).max(-1, keepdims=True)
    byte = np.maximum(np.where(amax > 0, np.frexp(amax)[1] - 1 + 127, 0) - down, 1)
    scale = np.exp2(byte - 127.0)
    codes = (blocks / scale).astype(np.float32).astype(dtype).astype(np.float64)
    return np.moveaxis((codes * scale).reshape(v.shape), -1, axis)


WIDE = False


def mx_kscale(k):
    if not WIDE:
        return np.ones(k)
    levels = np.array([10, -10, 5, -5, 0])
    if k % 512:
        return np.exp2(np.random.permutation(np.resize(levels, k // 32))).repeat(32)
    a = np.empty((k // 512, 16))
    for p in range(k // 512):
        a[p, :8] = np.random.permutation(np.resize(levels, 8))
        for g in range(8):
            far = levels[np.abs(levels - a[p, g]) >= 10]
            a[p, g + 8] = far[np.random.randint(len(far))]
    return np.exp2(a.ravel()).repeat(32)


def f64(x):
    return np.asarray(x).astype(np.float64)


def striped(idx):
    return np.tile(np.asarray(idx).reshape(-1, 16).T, (8, 1)).astype(np.uint16)


def unstriped(offs):
    return offs[:16].T.reshape(-1).astype(np.int64)


O, G, K, T, D, M = 4, 512, 4, 1024, 512, 256


def setup_inputs():
    n = np.random.standard_normal
    s = mx_kscale(D)[:, None]
    grid = lambda x: np.round(x * 32) / 32
    part = np.random.randint(1, 128 // K, (O, G, K)) / 64.0
    return {
        "xT": (grid(n((D, T))) * s).astype(np.float32),
        "w": (n((O, D, M)) / np.sqrt(O * D) / s).astype(np.float32),
        "part": np.tile(part.reshape(-1), (128, 1)).astype(np.float32),
        "bias": (0.3 * n((M, 1))).astype(np.float32),
        "offs": striped(np.random.randint(0, T, O * G * K)),
    }


def reference(xT, w, part, bias, offs):
    x = f64(xT)[:, unstriped(offs)] * f64(part)[:1]
    e = mxq(x.reshape(D, O, G, K).sum(-1), 0, "e4m3")
    wq = mxq(f64(w), 1, "e4m3")
    y = sum(wq[o].T @ e[:, o] for o in range(O))
    y = y + f64(bias)
    return y

from contextlib import ExitStack

import concourse.mybir as mybir
from concourse.masks import make_identity

O, G, J, T, D, M = 4, 512, 4, 1024, 512, 256
P = 128
FLOPS = 2 * O * D * M * G
BYTES = 4 * (D * T + O * D * M + O * G * J + M + M * G) + 2 * O * G * J

F32 = mybir.dt.float32
BF16 = mybir.dt.bfloat16
U32 = mybir.dt.uint32
U16 = mybir.dt.uint16
U8 = mybir.dt.uint8
FP8X4 = mybir.dt.float8_e4m3fn_x4
COPY = mybir.ActivationFunctionType.Copy
IDENTITY = mybir.ActivationFunctionType.Identity
MULT = mybir.AluOpType.mult
ADD = mybir.AluOpType.add


def tile_attend_deform_bias_kernel(tc, xT, w, part, bias, offs, out):
    nc = tc.nc
    with ExitStack() as ctx:
        held = ctx.enter_context(tc.tile_pool(name="held", bufs=1))
        ring = ctx.enter_context(tc.tile_pool(name="ring", bufs=3))
        fwd_ps = ctx.enter_context(tc.psum_pool(name="fwd_ps", bufs=4))
        back_ps = ctx.enter_context(tc.psum_pool(name="back_ps", bufs=2))
        acc_ps = ctx.enter_context(tc.psum_pool(name="acc_ps", bufs=1))

        lists = held.tile([P, O * G * J // 16], U16, name="lists")

        x_rows = xT.rearrange("(p u e) c -> u p e c", u=2, e=2)
        raws = {}

        def load_x(u):
            for h in range(2):
                raw = held.tile([P, 2, T // 2], F32, name="x_raw%d%d" % (u, h))
                nc.sync.dma_start(raw[:], x_rows[u][:, :, h * (T // 2) : (h + 1) * (T // 2)])
                raws[u, h] = raw

        load_x(0)
        nc.sync.dma_start(lists[:], offs)
        part_raw = held.tile([P, 512], F32, name="part_raw")
        nc.sync.dma_start(part_raw[:], part[0:8, :].rearrange("r (q c) -> (r q) c", c=512))
        load_x(1)
        w_raw = []
        for o in range(O):
            wr = held.tile([P, 4, M], F32, name="w_raw%d" % o)
            nc.sync.dma_start(wr[:], w[o].rearrange("(p t) m -> p t m", t=4))
            w_raw.append(wr)
        bias_col = held.tile([P, 2], F32, name="bias_col")
        nc.sync.dma_start(bias_col[:], bias.rearrange("(h p) x -> p (h x)", p=P))

        ident = held.tile([P, P], F32, name="ident")
        make_identity(nc, ident[:])

        windows = [held.tile([P, 2 * T], BF16, name="window%d" % u) for u in range(2)]

        def cast_x(u):
            for h in range(2):
                dst = windows[u][:, h * T : (h + 1) * T].rearrange("p (c e) -> p c e", e=2)
                srcv = raws[u, h][:].rearrange("p e c -> p c e")
                if h == 1:
                    nc.vector.tensor_copy(dst, srcv)
                else:
                    nc.scalar.activation(dst, srcv, COPY)

        cast_x(0)
        part_split = held.tile([P, J, P], F32, name="part_split")
        nc.scalar.activation(part_split[:], part_raw[:].rearrange("p (g j) -> p j g", j=J), COPY)
        part_bank = fwd_ps.tile([P, J, P], F32, name="bank")
        for j in range(J):
            nc.tensor.transpose(part_bank[:, j, :], part_split[:, j, :], ident[:])
        part_col = held.tile([P, J, 16], F32, name="part_col")
        nc.scalar.activation(part_col[:], part_bank[:, :, 0:16], COPY)
        cast_x(1)

        w_codes, w_scales, w_group = [], [], []
        for o in range(O):
            wg = held.tile([P, M, 4], BF16, name="w_group%d" % o, align_bytes=64)
            nc.gpsimd.tensor_scalar(wg[:], w_raw[o][:].rearrange("p t m -> p m t"), 1.0, 0.0, op0=MULT, op1=ADD)
            w_group.append(wg)
            w_codes.append(held.tile([P, M], U32, name="w_codes%d" % o, align_bytes=64))
            w_scales.append(held.tile([P, M], U8, name="w_scales%d" % o, align_bytes=64))

        def quant_w(o):
            nc.vector.quantize_mx(
                out=w_codes[o][:].bitcast(FP8X4), scales=w_scales[o][:],
                in_=w_group[o][:].rearrange("p m t -> p (m t)"))

        blocks = [(gb, o) for gb in range(4) for o in range(O)]
        words, banks, prods, backs, groups, quants, accs = {}, {}, {}, {}, {}, {}, {}

        def gather(i, u):
            gb, o = blocks[i]
            a = 128 * o + 32 * gb
            wd = ring.tile([P, J, 2 * P], BF16, name="words%d" % u)
            nc.vector.tensor_copy(
                wd[:].bitcast(U32).rearrange("p j g -> p g j"),
                windows[u][:].bitcast(U32).indirect(lists[:, a : a + 32]))
            words[i, u] = wd

        def forward(i):
            for half in range(2):
                bank = fwd_ps.tile([P, 2, 2, P], F32, name="bank")
                for jj in range(2):
                    for u in range(2):
                        nc.tensor.transpose(bank[:, jj, u, :], words[i, u][:, 2 * half + jj, :].bitcast(F32), ident[:])
                banks[i, half] = bank

        def product(i):
            gb, o = blocks[i]
            q = 4 * o + gb
            pr = ring.tile([P, J, 2, 2, P], F32, name="prod")
            for j in range(J):
                srcv = banks[i, j // 2][:, j % 2, :, :].bitcast(BF16).rearrange("p u (m e) -> p u e m", e=2)
                nc.scalar.activation(pr[:, j, :, :, :], srcv, COPY, scale=part_col[:, j, q : q + 1])
            prods[i] = pr

        def backward(i):
            bk = back_ps.tile([P, 4, P], F32, name="back")
            for t in range(4):
                for j in range(J):
                    nc.tensor.matmul(bk[:, t, :], prods[i][:, j, t // 2, t % 2, :], ident[:],
                                     start=(j == 0), stop=(j == J - 1), is_transpose=True)
            backs[i] = bk

        def round_e(i, on_vector):
            eg = ring.tile([P, P, 4], BF16, name="e_group", align_bytes=64)
            srcv = backs[i][:].rearrange("p t g -> p g t")
            if on_vector:
                nc.vector.tensor_copy(eg[:], srcv)
            else:
                nc.scalar.copy(eg[:], srcv)
            groups[i] = eg

        def quant_e(i):
            codes = ring.tile([P, P], U32, name="e_codes", align_bytes=64)
            scales = ring.tile([P, P], U8, name="e_scales", align_bytes=64)
            nc.vector.quantize_mx(out=codes[:].bitcast(FP8X4), scales=scales[:],
                                  in_=groups[i][:].rearrange("p g t -> p (g t)"))
            quants[i] = (codes, scales)

        def multiply(i):
            gb, o = blocks[i]
            codes, scales = quants[i]
            for m in range(2):
                if o == 0:
                    accs[m] = acc_ps.tile([P, P], F32, name="acc%d" % m)
                cols = slice(m * P, (m + 1) * P)
                nc.tensor.matmul_mx(
                    out=accs[m][:], lhsT=w_codes[o][:, cols].bitcast(FP8X4), lhsT_scale=w_scales[o][:, cols],
                    rhs=codes[:].bitcast(FP8X4), rhs_scale=scales[:], start=(o == 0), stop=(o == O - 1))
            if o == O - 1:
                for m in range(2):
                    res = ring.tile([P, P], F32, name="res%d" % m)
                    if m == 0 or i < n - 1:
                        nc.scalar.activation(res[:], accs[m][:], IDENTITY, bias=bias_col[:, m : m + 1])
                    else:
                        nc.vector.tensor_scalar(res[:], accs[m][:], bias_col[:, m : m + 1], None, op0=ADD)
                    nc.sync.dma_start(out[m * P : (m + 1) * P, gb * P : (gb + 1) * P], res[:])

        def forward_last(u):
            i = n - 1
            halves = []
            if u == 0:
                bank = fwd_ps.tile([P, J, P], F32, name="bank")
                halves = [bank]
                for j in range(J):
                    nc.tensor.transpose(bank[:, j, :], words[i, u][:, j, :].bitcast(F32), ident[:])
            else:
                for half in range(2):
                    bank = fwd_ps.tile([P, 2, P], F32, name="bank")
                    for jj in range(2):
                        nc.tensor.transpose(bank[:, jj, :], words[i, u][:, 2 * half + jj, :].bitcast(F32), ident[:])
                    halves.append(bank)
            banks[i, u] = halves

        def product_last(u):
            i = n - 1
            gb, o = blocks[i]
            q = 4 * o + gb
            pr = ring.tile([P, J, 2, P], F32, name="prod_last%d" % u)
            per = J // len(banks[i, u])
            for j in range(J):
                srcv = banks[i, u][j // per][:, j % per, :].bitcast(BF16).rearrange("p (m e) -> p e m", e=2)
                if j // per == 0:
                    nc.scalar.activation(pr[:, j, :, :], srcv, COPY, scale=part_col[:, j, q : q + 1])
                else:
                    nc.vector.tensor_scalar(pr[:, j, :, :], srcv, part_col[:, j, q : q + 1], None, op0=MULT)
            prods[i, u] = pr

        def backward_last(u):
            i = n - 1
            bk = back_ps.tile([P, 2, P], F32, name="back")
            for e in range(2):
                for j in range(J):
                    nc.tensor.matmul(bk[:, e, :], prods[i, u][:, j, e, :], ident[:],
                                     start=(j == 0), stop=(j == J - 1), is_transpose=True)
            backs[i, u] = bk

        def round_last(u):
            i = n - 1
            if u == 0:
                eg = ring.tile([P, P, 4], BF16, name="e_group", align_bytes=64)
                groups[i] = eg
            dst = groups[i][:, :, 2 * u : 2 * u + 2]
            srcv = backs[i, u][:].rearrange("p e g -> p g e")
            if u == 0:
                nc.scalar.copy(dst, srcv)
            else:
                nc.vector.tensor_copy(dst, srcv)

        n = len(blocks)
        gather(0, 0)
        gather(1, 0)
        gather(0, 1)
        gather(1, 1)
        forward(0)
        product(0)
        for i in range(1, n - 1):
            if i > 1:
                gather(i, 0)
                gather(i, 1)
            if i >= 2 and i % 4 == 2:
                round_e(i - 2, True)
            if 3 <= i < 3 + O:
                quant_w(i - 3)
            if i >= 3:
                quant_e(i - 3)
            forward(i)
            product(i)
            backward(i - 1)
            if i % 4 != 1:
                round_e(i - 1, False)
            if i >= 3:
                multiply(i - 3)
        gather(n - 1, 0)
        gather(n - 1, 1)
        forward_last(0)
        product_last(0)
        backward(n - 2)
        round_e(n - 2, False)
        quant_e(n - 4)
        multiply(n - 4)
        quant_e(n - 3)
        multiply(n - 3)
        forward_last(1)
        backward_last(0)
        product_last(1)
        round_last(0)
        quant_e(n - 2)
        multiply(n - 2)
        backward_last(1)
        round_last(1)
        quant_e(n - 1)
        multiply(n - 1)
